import numpy as np
import ml_dtypes


def mxq(x, axis, fmt="e4m3"):
    dtype, down = {"e4m3": (ml_dtypes.float8_e4m3fn, 7), "e5m2": (ml_dtypes.float8_e5m2, 14)}[fmt]
    v = np.moveaxis(np.asarray(x, np.float32).astype(ml_dtypes.bfloat16).astype(np.float64), axis, -1)
    blocks = v.reshape(v.shape[:-1] + (-1, 32))
    amax = np.abs(blocks).max(-1, keepdims=True)
    byte = np.maximum(np.where(amax > 0, np.frexp(amax)[1] - 1 + 127, 0) - down, 1)
    scale = np.exp2(byte - 127.0)
    codes = (blocks / scale).astype(np.float32).astype(dtype).astype(np.float64)
    return np.moveaxis((codes * scale).reshape(v.shape), -1, axis)


WIDE = False


def mx_kscale(k):
    if not WIDE:
        return np.ones(k)
    levels = np.array([10, -10, 5, -5, 0])
    if k % 512:
        return np.exp2(np.random.permutation(np.resize(levels, k // 32))).repeat(32)
    a = np.empty((k // 512, 16))
    for p in range(k // 512):
        a[p, :8] = np.random.permutation(np.resize(levels, 8))
        for g in range(8):
            far = levels[np.abs(levels - a[p, g]) >= 10]
            a[p, g + 8] = far[np.random.randint(len(far))]
    return np.exp2(a.ravel()).repeat(32)


def f64(x):
    return np.asarray(x).astype(np.float64)


def striped(idx):
    return np.tile(idx.reshape(-1, 16).T, (8, 1)).astype(np.uint16)


def unstriped(offs):
    return offs[:16].T.reshape(-1).astype(np.int64)


E2M1 = np.array([0.0, 0.5, 1.0, 1.5, 2.0, 3.0, 4.0, 6.0, -0.0, -0.5, -1.0, -1.5, -2.0, -3.0, -4.0, -6.0])


def pack_weight(w, fmt):
    k, n = w.shape
    w = f64(np.asarray(w, np.float32).astype(ml_dtypes.bfloat16)).reshape(k // 32, 32, n)
    amax = np.abs(w).max(1)
    if fmt == "e4m3":
        byte = np.frexp(amax)[1] - 1 + 127 - 7
    else:
        mant, ex = np.frexp(amax / 6.0)
        byte = np.where(mant > 0.5, ex, ex - 1) + 127
    byte = np.clip(np.where(amax > 0, byte, 1), 1, 254)
    scaled = (w * np.exp2(127.0 - byte)[:, None, :]).reshape(k, n).astype(np.float32)
    by_word = np.ascontiguousarray(scaled.reshape(k // 512, 128, 4, n).transpose(0, 1, 3, 2))
    if fmt == "e4m3":
        words = by_word.astype(ml_dtypes.float8_e4m3fn).view(np.uint8)
    else:
        c = by_word.astype(ml_dtypes.float4_e2m1fn).view(np.uint8) & 0xF
        words = (c[..., 0::2] | (c[..., 1::2] << 4)).reshape(k // 512, 128, 2 * n)
    return np.ascontiguousarray(words), np.ascontiguousarray(byte.astype(np.uint8).reshape(k // 512, 16, n))


def unpack_weight(words, scales, fmt):
    g, _, n = scales.shape
    words = np.ascontiguousarray(words).reshape(g, 128, n, -1)
    if fmt == "e4m3":
        vals = words.view(ml_dtypes.float8_e4m3fn).astype(np.float64)
    else:
        nib = np.empty((g, 128, n, 4), np.uint8)
        nib[..., 0::2] = words & 0xF
        nib[..., 1::2] = words >> 4
        vals = E2M1[nib]
    vals = vals * np.repeat(np.exp2(scales.astype(np.float64) - 127.0), 8, axis=1)[..., None]
    return vals.transpose(0, 1, 3, 2).reshape(g * 512, n)


def gelu(v):
    return 0.5 * v * (1.0 + np.tanh(np.sqrt(2.0 / np.pi) * (v + 0.044715 * v**3)))


def bf(x):
    return np.asarray(x, np.float32).astype(ml_dtypes.bfloat16)


def planes(Y):
    n, m = Y.shape
    b = f64(bf(Y)).reshape(n // 32, 32, m)
    amax = np.abs(b).max(1)
    byte = np.clip(np.where(amax > 0, np.frexp(amax)[1] - 1 + 127 - 7, 1), 1, 254)
    codes = (b * np.exp2(127.0 - byte)[:, None, :]).reshape(n, m).astype(np.float32).astype(ml_dtypes.float8_e4m3fn).view(np.uint8)
    words = codes.reshape(n // 512, 128, 4, m).transpose(0, 1, 3, 2)
    return np.ascontiguousarray(words), np.ascontiguousarray(byte.astype(np.uint8).reshape(n // 512, 16, m))


K, H, N, T, S, P = 1024, 1024, 512, 4096, 1024, 512


def setup_inputs():
    n = np.random.standard_normal
    s = mx_kscale(K)[:, None]
    u = mx_kscale(H)[:, None]
    d = {}
    d["tab_words"], d["tab_scales"] = pack_weight(n((K, T)) * s, "e4m3")
    d["offs"] = striped(np.random.permutation(T)[:S])
    d["pos1"] = striped(np.random.permutation(S)[:P])
    d["pos2"] = striped(np.random.permutation(S)[:P])
    d["w1"] = (1.2 * n((K, H)) / K**0.5 / s).astype(np.float32)
    d["gain"] = (np.exp(0.3 * n(H)) * u[:, 0]).astype(np.float32)
    d["w4_words"], d["w4_scales"] = pack_weight(n((H, N)) / H**0.5 / u, "e2m1")
    d["wk"] = (0.8 * n((K, N)) / K**0.5 / s).astype(np.float32)
    d["leadm"] = (n((N, P)) * np.exp(0.8 * n(N))[:, None]).astype(np.float32)
    return d


def reference(tab_words, tab_scales, offs, pos1, pos2, w1, gain, w4_words, w4_scales, wk, leadm):
    v = unpack_weight(tab_words, tab_scales, "e4m3")[:, unstriped(offs)]
    w4 = unpack_weight(w4_words, w4_scales, "e2m1")
    q = mxq(f64(w1), 0, "e4m3").T @ v
    h = f64(gain)[:, None] * np.log(1.0 + q * q)
    hq = mxq(h, 0, "e4m3")
    g2 = w4.T @ hq + mxq(f64(wk), 0, "e4m3").T @ v
    top = np.maximum(g2[:, unstriped(pos1)], g2[:, unstriped(pos2)])
    y = f64(leadm) * top
    words, scales = planes(y)
    return y, words, scales

@@ -1,0 +1,313 @@
+from contextlib import ExitStack
+
+import concourse.mybir as mybir
+
+K, H, N, T, S, PAIRS = 1024, 1024, 512, 4096, 1024, 512
+FLOPS = 2 * (K * H * S + H * N * S + K * N * S)
+
+F32 = mybir.dt.float32
+BF16 = mybir.dt.bfloat16
+I32 = mybir.dt.int32
+U32 = mybir.dt.uint32
+U16 = mybir.dt.uint16
+U8 = mybir.dt.uint8
+FP8X4 = mybir.dt.float8_e4m3fn_x4
+FP4X4 = mybir.dt.float4_e2m1fn_x4
+ACT = mybir.ActivationFunctionType
+ALU = mybir.AluOpType
+
+P = 128
+PACK = 4
+PASS = P * PACK
+HALF = 512
+CHUNK = 128
+CHUNKS = S // CHUNK
+BANKS = 8
+
+
+def tile_list_spindle_lead_scores_kernel(
+    tc, tab_words, tab_scales, offs, pos1, pos2, w1, gain, w4_words, w4_scales, wk, leadm, out_0, out_1, out_2
+):
+    nc = tc.nc
+    with ExitStack() as ctx:
+        keep = ctx.enter_context(tc.tile_pool(name="keep", bufs=1))
+        ring = ctx.enter_context(tc.tile_pool(name="ring", bufs=3))
+        psum = ctx.enter_context(tc.psum_pool(name="psum", bufs=1))
+
+        def kept(shape, dtype, name):
+            return keep.tile(shape, dtype, name=name, tag=name, align_bytes=64)
+
+        def bank(i):
+            return psum.tile([P, PACK, CHUNK], F32, name="bank%d" % i)
+
+        offs_sb = keep.tile([P, S // 16], U16, name="offs_sb")
+        pos1_sb = keep.tile([P, PAIRS // 16], U16, name="pos1_sb")
+        pos2_sb = keep.tile([P, PAIRS // 16], U16, name="pos2_sb")
+        table_rows = kept([P, 2, T // 4], I32, "table_rows")
+        planes_at = kept([P, (2 * S + 2 * N) // 4], I32, "planes_at")
+        w4_rows = kept([P, 2, N // 4], I32, "w4_rows")
+        one = kept([P, 1], F32, "one")
+        warm = kept([P, 1], F32, "warm")
+        nc.gpsimd.memset(table_rows[:, 1, :], 0)
+        nc.vector.memset(table_rows[:, 0, :], 0)
+        nc.vector.memset(w4_rows[:], 0)
+        nc.vector.memset(one[:], 1.0)
+        nc.vector.memset(planes_at[:], 0)
+        nc.scalar.activation(out=warm[:], in_=one[:], func=ACT.Ln)
+
+        def load_weight(raw, w, a, b):
+            rows = w[a * PASS : (a + 1) * PASS, b * PASS : (b + 1) * PASS]
+            nc.sync.dma_start(out=raw, in_=rows.rearrange("(p j) c -> p j c", j=PACK))
+            return raw
+
+        w1_raw = {}
+        w1_raw[0, 0] = load_weight(kept([P, PACK, PASS], F32, "w1_first")[:], w1, 0, 0)
+        nc.sync.dma_start(out=table_rows[0:P:8, :, :], in_=tab_scales.rearrange("a q t -> q a t").bitcast(I32))
+        nc.sync.dma_start(out=w4_rows[0:P:8, :, :], in_=w4_scales.rearrange("a q n -> q a n").bitcast(I32))
+        nc.sync.dma_start(offs_sb[:], offs)
+        nc.sync.dma_start(pos1_sb[:], pos1)
+        nc.sync.dma_start(pos2_sb[:], pos2)
+        w4_raw = kept([P, 2, N // 2], I32, "w4_raw")
+        nc.sync.dma_start(out=w4_raw[:], in_=w4_words.rearrange("a p c -> p a c").bitcast(I32))
+        gain_sb = kept([P, 2, PACK], F32, "gain_sb")
+        nc.scalar.dma_start(out=gain_sb[:], in_=gain.rearrange("(b p t) -> p b t", b=2, t=PACK))
+        table = []
+        for a in range(2):
+            words = kept([P, T], I32, "table%d" % a)
+            nc.sync.dma_start(out=words[:], in_=tab_words[a].rearrange("p t i -> p (t i)").bitcast(I32))
+            table.append(words)
+        w1_raw[1, 0] = load_weight(kept([P, PACK, PASS], F32, "staging1")[:], w1, 1, 0)
+
+        def round_weight(raw, scalar_share):
+            grouped = ring.tile([P, PASS * PACK], BF16, name="grouped", align_bytes=64)
+            dst = grouped[:].rearrange("p (t m j) -> p m j t", t=PACK, j=PACK)
+            src = raw.rearrange("p j (m t) -> p m j t", t=PACK)
+            if scalar_share > 0:
+                nc.scalar.copy(out=dst[:, :scalar_share, :, :], in_=src[:, :scalar_share, :, :])
+            if scalar_share < P:
+                nc.vector.tensor_copy(out=dst[:, scalar_share:, :, :], in_=src[:, scalar_share:, :, :])
+            return grouped
+
+        def quantize_weight(grouped, name):
+            codes = kept([P, PASS], U32, name + "_codes")
+            plane = kept([P, PASS], U8, name + "_plane")
+            nc.vector.quantize_mx(out=codes[:].bitcast(FP8X4), scales=plane[:], in_=grouped[:])
+            return codes, plane
+
+        picked_rows = kept([P, 2, S // 4], I32, "picked_rows")
+        rows_out = kept([P, (2 * S + 2 * N) // 4], I32, "staging0")
+        nc.vector.tensor_copy(
+            out=rows_out[:, 2 * S // 4 :].bitcast(U8).rearrange("p (a t m) -> p a m t", a=2, t=PACK),
+            in_=w4_rows[:].bitcast(U8).rearrange("p a (m t) -> p a m t", t=PACK),
+        )
+        for a in range(2):
+            nc.vector.tensor_copy(picked_rows[:, a, :].bitcast(U8), table_rows[:, a, :].bitcast(U8).indirect(offs_sb[:]))
+        nc.vector.tensor_copy(out=rows_out[:, : 2 * S // 4], in_=picked_rows[:].rearrange("p a s -> p (a s)"))
+        for r in range(4):
+            nc.scalar.dma_start(out=planes_at[r:P:32, :], in_=rows_out[8 * r : P : 32, :])
+        plane_bytes = planes_at[:].bitcast(U8)
+
+        w1_q = {}
+        w1_q[0, 0] = quantize_weight(round_weight(w1_raw[0, 0], P), "w1_00")
+        w1_raw[0, 1] = load_weight(kept([P, PACK, PASS], F32, "staging0")[:], w1, 0, 1)
+
+        w4_codes = kept([P, 2, 2 * N], U8, "w4_codes")
+        for b in range(2):
+            nc.vector.tensor_copy(
+                out=w4_codes[:, b, :].rearrange("p (t m e) -> p m t e", t=PACK, e=2),
+                in_=w4_raw[:, b, :].bitcast(U8).rearrange("p (m t e) -> p m t e", t=PACK, e=2),
+            )
+
+        def half_list(h):
+            return offs_sb[:, h * HALF // 16 : (h + 1) * HALF // 16]
+
+        v_words = {}
+
+        def gather_words(a, h):
+            v_words[a, h] = kept([P, HALF], U32, "v_words%d%d" % (a, h))
+            nc.vector.tensor_copy(v_words[a, h][:], table[a][:].bitcast(U32).indirect(half_list(h)))
+
+        for h in range(2):
+            gather_words(0, h)
+
+        w1_raw[1, 1] = load_weight(kept([P, PACK, PASS], F32, "table0")[:], w1, 1, 1)
+        for h in range(2):
+            gather_words(1, h)
+        wk_raw = {0: load_weight(kept([P, PACK, PASS], F32, "table1")[:], wk, 0, 0)}
+        w1_q[1, 0] = quantize_weight(round_weight(w1_raw[1, 0], 40), "w1_10")
+        wk_raw[1] = load_weight(kept([P, PACK, PASS], F32, "staging1")[:], wk, 1, 0)
+
+        def v_operand(a, h, cols):
+            return v_words[a, h][:, cols].bitcast(FP8X4), plane_bytes[:, a * S + h * HALF + cols.start : a * S + h * HALF + cols.stop]
+
+        def q_pass(acc, a, b, c):
+            h, cols = c // PACK, slice(c % PACK * CHUNK, (c % PACK + 1) * CHUNK)
+            codes, plane = w1_q[a, b]
+            rhs, rhs_scale = v_operand(a, h, cols)
+            for t in range(PACK):
+                nc.tensor.matmul_mx(
+                    out=acc[:, t, :],
+                    lhsT=codes[:, t * P : (t + 1) * P].bitcast(FP8X4),
+                    lhsT_scale=plane[:, t * P : (t + 1) * P],
+                    rhs=rhs,
+                    rhs_scale=rhs_scale,
+                    start=(a == 0 and t == 0),
+                    stop=(a == 1 and t == PACK - 1),
+                )
+
+        h_codes = {(b, h): kept([P, HALF], U32, "h_codes%d%d" % (b, h)) for b in range(2) for h in range(2)}
+        h_plane = {(b, h): kept([P, HALF], U8, "h_plane%d%d" % (b, h)) for b in range(2) for h in range(2)}
+
+        def log_energy(acc, logs):
+            squares = ring.tile([P, CHUNK, PACK], F32, name="squares")
+            nc.scalar.activation(out=squares[:], in_=acc[:].rearrange("p t j -> p j t"), func=ACT.Square)
+            nc.scalar.activation(out=logs, in_=squares[:], func=ACT.Ln, bias=1.0)
+
+        def apply_gain(logs, b):
+            width = logs.shape[1]
+            h_bf = ring.tile([P, width, PACK], BF16, name="h_bf", align_bytes=64)
+            nc.vector.tensor_tensor(
+                out=h_bf[:], in0=logs, in1=gain_sb[:, b : b + 1, :].to_broadcast([P, width, PACK]), op=ALU.mult
+            )
+            return h_bf
+
+        def quantize_features(h_bf, b, j0):
+            h, cols = j0 // HALF, slice(j0 % HALF, j0 % HALF + h_bf.shape[1])
+            nc.vector.quantize_mx(
+                out=h_codes[b, h][:, cols].bitcast(FP8X4),
+                scales=h_plane[b, h][:, cols],
+                in_=h_bf[:].rearrange("p j t -> p (j t)"),
+            )
+
+        g2_acc = {}
+
+        def g2_w4_pass(t, h, b):
+            nc.tensor.matmul_mx(
+                out=g2_acc[t, h][:].rearrange("p t j -> p (t j)"),
+                lhsT=w4_codes[:, b, 2 * t * P : 2 * (t + 1) * P].bitcast(FP4X4),
+                lhsT_scale=plane_bytes[:, 2 * S + b * N + t * P : 2 * S + b * N + (t + 1) * P],
+                rhs=h_codes[b, h][:].bitcast(FP8X4),
+                rhs_scale=h_plane[b, h][:],
+                start=(b == 0),
+                stop=(b == 1),
+            )
+
+        def g2_wk_pass(t, h, a):
+            codes, plane = wk_q[a]
+            rhs, rhs_scale = v_operand(a, h, slice(0, HALF))
+            nc.tensor.matmul_mx(
+                out=g2_acc[t, h][:].rearrange("p t j -> p (t j)"),
+                lhsT=codes[:, t * P : (t + 1) * P].bitcast(FP8X4),
+                lhsT_scale=plane[:, t * P : (t + 1) * P],
+                rhs=rhs,
+                rhs_scale=rhs_scale,
+                start=False,
+                stop=False,
+            )
+
+        q_acc = [bank(c) for c in range(CHUNKS)]
+        for c in range(CHUNKS):
+            q_pass(q_acc[c], 0, 0, c)
+        for a in range(2):
+            w1_q[a, 1] = quantize_weight(round_weight(w1_raw[a, 1], 0), "w1_%d1" % a)
+        lead = kept([P, PACK, PAIRS], F32, "staging0")
+        nc.sync.dma_start(out=lead[:], in_=leadm.rearrange("(p t) m -> p t m", t=PACK))
+        pending = []
+        for c in range(CHUNKS):
+            q_pass(q_acc[c], 1, 0, c)
+            if c % 2 == 0:
+                logs = ring.tile([P, 2 * CHUNK, PACK], F32, name="logs", bufs=4)
+            log_energy(q_acc[c], logs[:, c % 2 * CHUNK : (c % 2 + 1) * CHUNK, :])
+            if c % 2 == 1:
+                h_bf = apply_gain(logs[:], 0)
+                if pending:
+                    quantize_features(*pending.pop())
+                pending.append((h_bf, 0, (c - 1) * CHUNK))
+
+        wk_q = {}
+        for c in range(CHUNKS):
+            acc = bank(c % 2)
+            for a in range(2):
+                q_pass(acc, a, 1, c)
+            if c % 2 == 0:
+                logs = ring.tile([P, 2 * CHUNK, PACK], F32, name="logs", bufs=4)
+            part = logs[:, c % 2 * CHUNK : (c % 2 + 1) * CHUNK, :]
+            log_energy(acc, part)
+            if c >= CHUNKS - 2:
+                h_bf = apply_gain(part, 1)
+                quantize_features(*pending.pop())
+                pending.append((h_bf, 1, c * CHUNK))
+            elif c % 2 == 1:
+                h_bf = apply_gain(logs[:], 1)
+                quantize_features(*pending.pop())
+                pending.append((h_bf, 1, (c - 1) * CHUNK))
+            if c < 2:
+                grouped = round_weight(wk_raw[c], 0)
+                wk_q[c] = quantize_weight(grouped, "wk_%d" % c)
+            if c in (1, 2):
+                for t in range(PACK - 1):
+                    g2_acc[t, c - 1] = bank(2 + 2 * t + c - 1)
+                    g2_w4_pass(t, c - 1, 0)
+            if 3 <= c < 7:
+                for t in range(PACK - 1):
+                    g2_wk_pass(t, (c - 3) % 2, (c - 3) // 2)
+            if c == CHUNKS - 1:
+                for t in range(PACK - 1):
+                    g2_w4_pass(t, 0, 1)
+        quantize_features(*pending.pop())
+        for t in range(PACK - 1):
+            g2_w4_pass(t, 1, 1)
+        t = PACK - 1
+        for h in range(2):
+            g2_acc[t, h] = bank(h)
+            g2_w4_pass(t, h, 0)
+            for a in range(2):
+                g2_wk_pass(t, h, a)
+            g2_w4_pass(t, h, 1)
+
+        g2 = [kept([P, S], F32, "g2_%d" % t) for t in range(PACK)]
+        for t, h in [(0, 0), (1, 0), (0, 1), (1, 1), (2, 0), (2, 1), (3, 0), (3, 1)]:
+            nc.scalar.copy(out=g2[t][:, h * HALF : (h + 1) * HALF], in_=g2_acc[t, h][:].rearrange("p t j -> p (t j)"))
+
+        y = kept([P, PACK, PAIRS], F32, "y")
+        y_rows = out_0.rearrange("(p t) m -> p t m", t=PACK)
+        y_codes = kept([P, PAIRS], I32, "y_codes")
+        y_plane = kept([P, PAIRS // 4], I32, "y_plane")
+
+        def pairs(t, m0, m1):
+            left = ring.tile([P, m1 - m0], F32, name="left")
+            right = ring.tile([P, m1 - m0], F32, name="right")
+            top = ring.tile([P, m1 - m0], F32, name="top")
+            nc.vector.tensor_copy(left[:], g2[t][:].indirect(pos1_sb[:, m0 // 16 : m1 // 16]))
+            nc.vector.tensor_copy(right[:], g2[t][:].indirect(pos2_sb[:, m0 // 16 : m1 // 16]))
+            nc.vector.tensor_tensor(out=top[:], in0=left[:], in1=right[:], op=ALU.max)
+            nc.vector.tensor_tensor(out=y[:, t, m0:m1], in0=top[:], in1=lead[:, t, m0:m1], op=ALU.mult)
+            nc.sync.dma_start(out=y_rows[:, t, m0:m1], in_=y[:, t, m0:m1])
+
+        def planes(m0, m1, on_scalar):
+            y_bf = kept([P, m1 - m0, PACK], BF16, "y_bf%d" % m0)
+            dst = y_bf[:].rearrange("p (c i) t -> p c t i", i=4)
+            src = y[:, :, m0:m1].rearrange("p t (c i) -> p c t i", i=4)
+            if on_scalar:
+                nc.scalar.copy(out=dst, in_=src)
+            else:
+                nc.vector.tensor_copy(out=dst, in_=src)
+            nc.vector.quantize_mx(
+                out=y_codes[:, m0:m1].bitcast(FP8X4),
+                scales=y_plane[:].bitcast(U8)[:, m0:m1],
+                in_=y_bf[:].rearrange("p m t -> p (m t)"),
+            )
+            nc.sync.dma_start(
+                out=out_1[0, :, m0:m1, :].rearrange("p m t -> p (m t)").bitcast(I32), in_=y_codes[:, m0:m1]
+            )
+
+        for t in range(PACK - 1):
+            pairs(t, 0, PAIRS)
+        pairs(PACK - 1, 0, PAIRS // 2)
+        pairs(PACK - 1, PAIRS // 2, PAIRS)
+        planes(0, PAIRS // 2, True)
+        planes(PAIRS // 2, PAIRS, False)
+        for q in range(4):
+            nc.scalar.dma_start(
+                out=out_2[0, 4 * q : 4 * q + 4, :].bitcast(I32), in_=y_plane[32 * q : 32 * q + 4, :]
+            )

@@ -43,45 +43,52 @@ def tile_list_spindle_lead_scores_kernel(
         offs_sb = keep.tile([P, S // 16], U16, name="offs_sb")
         pos1_sb = keep.tile([P, PAIRS // 16], U16, name="pos1_sb")
         pos2_sb = keep.tile([P, PAIRS // 16], U16, name="pos2_sb")
-        table_rows = kept([P, 2, T // 4], I32, "table_rows")
-        planes_at = kept([P, (2 * S + 2 * N) // 4], I32, "planes_at")
-        w4_rows = kept([P, 2, N // 4], I32, "w4_rows")
+        table_planes = kept([P, T // 4], I32, "table_planes")
+        w4_planes_raw = kept([P, 2, N // 4], I32, "w4_planes_raw")
         one = kept([P, 1], F32, "one")
         warm = kept([P, 1], F32, "warm")
-        nc.gpsimd.memset(table_rows[:, 1, :], 0)
-        nc.vector.memset(table_rows[:, 0, :], 0)
-        nc.vector.memset(w4_rows[:], 0)
         nc.vector.memset(one[:], 1.0)
-        nc.vector.memset(planes_at[:], 0)
+        nc.vector.memset(table_planes[:], 0)
+        nc.vector.memset(w4_planes_raw[:], 0)
         nc.scalar.activation(out=warm[:], in_=one[:], func=ACT.Ln)
 
-        def load_weight(raw, w, a, b):
+        def load_weight(w, a, b, buffer):
+            raw = kept([P, PACK, PASS], F32, buffer)
             rows = w[a * PASS : (a + 1) * PASS, b * PASS : (b + 1) * PASS]
-            nc.sync.dma_start(out=raw, in_=rows.rearrange("(p j) c -> p j c", j=PACK))
-            return raw
+            nc.sync.dma_start(out=raw[:], in_=rows.rearrange("(p j) c -> p j c", j=PACK))
+            return raw[:]
 
         w1_raw = {}
-        w1_raw[0, 0] = load_weight(kept([P, PACK, PASS], F32, "w1_first")[:], w1, 0, 0)
-        nc.sync.dma_start(out=table_rows[0:P:8, :, :], in_=tab_scales.rearrange("a q t -> q a t").bitcast(I32))
-        nc.sync.dma_start(out=w4_rows[0:P:8, :, :], in_=w4_scales.rearrange("a q n -> q a n").bitcast(I32))
+        w1_raw[0, 0] = load_weight(w1, 0, 0, "staging0")
         nc.sync.dma_start(offs_sb[:], offs)
-        nc.sync.dma_start(pos1_sb[:], pos1)
-        nc.sync.dma_start(pos2_sb[:], pos2)
+        w1_raw[1, 0] = load_weight(w1, 1, 0, "staging1")
         w4_raw = kept([P, 2, N // 2], I32, "w4_raw")
         nc.sync.dma_start(out=w4_raw[:], in_=w4_words.rearrange("a p c -> p a c").bitcast(I32))
-        gain_sb = kept([P, 2, PACK], F32, "gain_sb")
-        nc.scalar.dma_start(out=gain_sb[:], in_=gain.rearrange("(b p t) -> p b t", b=2, t=PACK))
-        table = []
+        nc.sync.dma_start(pos1_sb[:], pos1)
+        nc.sync.dma_start(pos2_sb[:], pos2)
+        table = {}
         for a in range(2):
-            words = kept([P, T], I32, "table%d" % a)
-            nc.sync.dma_start(out=words[:], in_=tab_words[a].rearrange("p t i -> p (t i)").bitcast(I32))
-            table.append(words)
-        w1_raw[1, 0] = load_weight(kept([P, PACK, PASS], F32, "staging1")[:], w1, 1, 0)
+            table[a] = kept([P, T], I32, "table%d" % a)
+            nc.sync.dma_start(out=table[a][:], in_=tab_words[a].rearrange("p t i -> p (t i)").bitcast(I32))
+        for q in range(4):
+            for a in range(2):
+                queue = nc.gpsimd if q == 3 else nc.scalar
+                queue.dma_start(
+                    out=table_planes[32 * q + 4 * a : 32 * q + 4 * a + 4, :],
+                    in_=tab_scales[a, 4 * q : 4 * q + 4, :].bitcast(I32),
+                )
+        for q in range(4):
+            nc.gpsimd.dma_start(
+                out=w4_planes_raw[32 * q : 32 * q + 4, :, :],
+                in_=w4_scales[:, 4 * q : 4 * q + 4, :].rearrange("a r n -> r a n").bitcast(I32),
+            )
+        gain_sb = kept([P, 2, PACK], F32, "gain_sb")
+        nc.gpsimd.dma_start(out=gain_sb[:], in_=gain.rearrange("(b p t) -> p b t", b=2, t=PACK))
 
         def round_weight(raw, scalar_share):
             grouped = ring.tile([P, PASS * PACK], BF16, name="grouped", align_bytes=64)
-            dst = grouped[:].rearrange("p (t m j) -> p m j t", t=PACK, j=PACK)
-            src = raw.rearrange("p j (m t) -> p m j t", t=PACK)
+            dst = grouped[:].rearrange("p (t m j) -> p m t j", t=PACK, j=PACK)
+            src = raw.rearrange("p j (m t) -> p m t j", t=PACK)
             if scalar_share > 0:
                 nc.scalar.copy(out=dst[:, :scalar_share, :, :], in_=src[:, :scalar_share, :, :])
             if scalar_share < P:
@@ -94,29 +101,25 @@ def tile_list_spindle_lead_scores_kernel(
             nc.vector.quantize_mx(out=codes[:].bitcast(FP8X4), scales=plane[:], in_=grouped[:])
             return codes, plane
 
-        picked_rows = kept([P, 2, S // 4], I32, "picked_rows")
-        rows_out = kept([P, (2 * S + 2 * N) // 4], I32, "staging0")
-        nc.vector.tensor_copy(
-            out=rows_out[:, 2 * S // 4 :].bitcast(U8).rearrange("p (a t m) -> p a m t", a=2, t=PACK),
-            in_=w4_rows[:].bitcast(U8).rearrange("p a (m t) -> p a m t", t=PACK),
-        )
-        for a in range(2):
-            nc.vector.tensor_copy(picked_rows[:, a, :].bitcast(U8), table_rows[:, a, :].bitcast(U8).indirect(offs_sb[:]))
-        nc.vector.tensor_copy(out=rows_out[:, : 2 * S // 4], in_=picked_rows[:].rearrange("p a s -> p (a s)"))
-        for r in range(4):
-            nc.scalar.dma_start(out=planes_at[r:P:32, :], in_=rows_out[8 * r : P : 32, :])
-        plane_bytes = planes_at[:].bitcast(U8)
-
         w1_q = {}
-        w1_q[0, 0] = quantize_weight(round_weight(w1_raw[0, 0], P), "w1_00")
-        w1_raw[0, 1] = load_weight(kept([P, PACK, PASS], F32, "staging0")[:], w1, 0, 1)
+        for a in range(2):
+            w1_q[a, 0] = quantize_weight(round_weight(w1_raw[a, 0], P), "w1_%d0" % a)
+            w1_raw[a, 1] = load_weight(w1, a, 1, "staging%d" % a)
+
+        v_planes = kept([P, S], U8, "v_planes")
+        nc.vector.tensor_copy(v_planes[:], table_planes[:].bitcast(U8).indirect(offs_sb[:]))
 
         w4_codes = kept([P, 2, 2 * N], U8, "w4_codes")
+        w4_planes = kept([P, 2, N], U8, "w4_planes")
         for b in range(2):
             nc.vector.tensor_copy(
-                out=w4_codes[:, b, :].rearrange("p (t m e) -> p m t e", t=PACK, e=2),
-                in_=w4_raw[:, b, :].bitcast(U8).rearrange("p (m t e) -> p m t e", t=PACK, e=2),
+                out=w4_codes[:, b, :].rearrange("p (t m e) -> p t m e", t=PACK, e=2),
+                in_=w4_raw[:, b, :].bitcast(U8).rearrange("p (m t e) -> p t m e", t=PACK, e=2),
             )
+        nc.vector.tensor_copy(
+            out=w4_planes[:].rearrange("p a (t m) -> p a t m", t=PACK),
+            in_=w4_planes_raw[:].bitcast(U8).rearrange("p a (m t) -> p a t m", t=PACK),
+        )
 
         def half_list(h):
             return offs_sb[:, h * HALF // 16 : (h + 1) * HALF // 16]
@@ -127,18 +130,14 @@ def tile_list_spindle_lead_scores_kernel(
             v_words[a, h] = kept([P, HALF], U32, "v_words%d%d" % (a, h))
             nc.vector.tensor_copy(v_words[a, h][:], table[a][:].bitcast(U32).indirect(half_list(h)))
 
+        wk_raw = {}
         for h in range(2):
             gather_words(0, h)
-
-        w1_raw[1, 1] = load_weight(kept([P, PACK, PASS], F32, "table0")[:], w1, 1, 1)
-        for h in range(2):
-            gather_words(1, h)
-        wk_raw = {0: load_weight(kept([P, PACK, PASS], F32, "table1")[:], wk, 0, 0)}
-        w1_q[1, 0] = quantize_weight(round_weight(w1_raw[1, 0], 40), "w1_10")
-        wk_raw[1] = load_weight(kept([P, PACK, PASS], F32, "staging1")[:], wk, 1, 0)
+        wk_raw[0] = load_weight(wk, 0, 0, "table0")
 
         def v_operand(a, h, cols):
-            return v_words[a, h][:, cols].bitcast(FP8X4), plane_bytes[:, a * S + h * HALF + cols.start : a * S + h * HALF + cols.stop]
+            at = slice(h * HALF + cols.start, h * HALF + cols.stop)
+            return v_words[a, h][:, cols].bitcast(FP8X4), v_planes[4 * a :, at]
 
         def q_pass(acc, a, b, c):
             h, cols = c // PACK, slice(c % PACK * CHUNK, (c % PACK + 1) * CHUNK)
@@ -185,7 +184,7 @@ def tile_list_spindle_lead_scores_kernel(
             nc.tensor.matmul_mx(
                 out=g2_acc[t, h][:].rearrange("p t j -> p (t j)"),
                 lhsT=w4_codes[:, b, 2 * t * P : 2 * (t + 1) * P].bitcast(FP4X4),
-                lhsT_scale=plane_bytes[:, 2 * S + b * N + t * P : 2 * S + b * N + (t + 1) * P],
+                lhsT_scale=w4_planes[:, b, t * P : (t + 1) * P],
                 rhs=h_codes[b, h][:].bitcast(FP8X4),
                 rhs_scale=h_plane[b, h][:],
                 start=(b == 0),
@@ -208,6 +207,9 @@ def tile_list_spindle_lead_scores_kernel(
         q_acc = [bank(c) for c in range(CHUNKS)]
         for c in range(CHUNKS):
             q_pass(q_acc[c], 0, 0, c)
+        for h in range(2):
+            gather_words(1, h)
+        wk_raw[1] = load_weight(wk, 1, 0, "table1")
         for a in range(2):
             w1_q[a, 1] = quantize_weight(round_weight(w1_raw[a, 1], 0), "w1_%d1" % a)
         lead = kept([P, PACK, PAIRS], F32, "staging0")
@@ -286,8 +288,8 @@ def tile_list_spindle_lead_scores_kernel(
 
         def planes(m0, m1, on_scalar):
             y_bf = kept([P, m1 - m0, PACK], BF16, "y_bf%d" % m0)
-            dst = y_bf[:].rearrange("p (c i) t -> p c t i", i=4)
-            src = y[:, :, m0:m1].rearrange("p t (c i) -> p c t i", i=4)
+            dst = y_bf[:]
+            src = y[:, :, m0:m1].rearrange("p t m -> p m t")
             if on_scalar:
                 nc.scalar.copy(out=dst, in_=src)
             else:

@@ -85,9 +85,11 @@ def tile_list_spindle_lead_scores_kernel(
         gain_sb = kept([P, 2, PACK], F32, "gain_sb")
         nc.gpsimd.dma_start(out=gain_sb[:], in_=gain.rearrange("(b p t) -> p b t", b=2, t=PACK))
 
-        def round_weight(raw, scalar_share):
-            grouped = ring.tile([P, PASS * PACK], BF16, name="grouped", align_bytes=64)
-            dst = grouped[:].rearrange("p (t m j) -> p m t j", t=PACK, j=PACK)
+        def round_weight(raw, scalar_share, grouped=None):
+            if grouped is None:
+                fresh = ring.tile([P, PASS * PACK], BF16, name="grouped", align_bytes=64)
+                grouped = fresh[:]
+            dst = grouped.rearrange("p (t m j) -> p m t j", t=PACK, j=PACK)
             src = raw.rearrange("p j (m t) -> p m t j", t=PACK)
             if scalar_share > 0:
                 nc.scalar.copy(out=dst[:, :scalar_share, :, :], in_=src[:, :scalar_share, :, :])
@@ -98,7 +100,7 @@ def tile_list_spindle_lead_scores_kernel(
         def quantize_weight(grouped, name):
             codes = kept([P, PASS], U32, name + "_codes")
             plane = kept([P, PASS], U8, name + "_plane")
-            nc.vector.quantize_mx(out=codes[:].bitcast(FP8X4), scales=plane[:], in_=grouped[:])
+            nc.vector.quantize_mx(out=codes[:].bitcast(FP8X4), scales=plane[:], in_=grouped)
             return codes, plane
 
         w1_q = {}
@@ -110,30 +112,30 @@ def tile_list_spindle_lead_scores_kernel(
         nc.vector.tensor_copy(v_planes[:], table_planes[:].bitcast(U8).indirect(offs_sb[:]))
 
         w4_codes = kept([P, 2, 2 * N], U8, "w4_codes")
-        w4_planes = kept([P, 2, N], U8, "w4_planes")
         for b in range(2):
             nc.vector.tensor_copy(
                 out=w4_codes[:, b, :].rearrange("p (t m e) -> p t m e", t=PACK, e=2),
                 in_=w4_raw[:, b, :].bitcast(U8).rearrange("p (m t e) -> p t m e", t=PACK, e=2),
             )
-        nc.vector.tensor_copy(
-            out=w4_planes[:].rearrange("p a (t m) -> p a t m", t=PACK),
-            in_=w4_planes_raw[:].bitcast(U8).rearrange("p a (m t) -> p a t m", t=PACK),
-        )
 
         def half_list(h):
             return offs_sb[:, h * HALF // 16 : (h + 1) * HALF // 16]
 
-        v_words = {}
+        v_all = kept([P, 2 * S], U32, "table_planes")
+        v_words = {(a, h): v_all[:, a * S + h * HALF : a * S + (h + 1) * HALF] for a in range(2) for h in range(2)}
 
         def gather_words(a, h):
-            v_words[a, h] = kept([P, HALF], U32, "v_words%d%d" % (a, h))
-            nc.vector.tensor_copy(v_words[a, h][:], table[a][:].bitcast(U32).indirect(half_list(h)))
+            nc.vector.tensor_copy(v_words[a, h], table[a][:].bitcast(U32).indirect(half_list(h)))
 
         wk_raw = {}
         for h in range(2):
             gather_words(0, h)
-        wk_raw[0] = load_weight(wk, 0, 0, "table0")
+        w4_planes = kept([P, 2, N], U8, "table0")
+        nc.vector.tensor_copy(
+            out=w4_planes[:].rearrange("p a (t m) -> p a t m", t=PACK),
+            in_=w4_planes_raw[:].bitcast(U8).rearrange("p a (m t) -> p a t m", t=PACK),
+        )
+        wk_raw[0] = load_weight(wk, 0, 0, "w4_planes_raw")
 
         def v_operand(a, h, cols):
             at = slice(h * HALF + cols.start, h * HALF + cols.stop)
@@ -209,16 +211,18 @@ def tile_list_spindle_lead_scores_kernel(
             q_pass(q_acc[c], 0, 0, c)
         for h in range(2):
             gather_words(1, h)
-        wk_raw[1] = load_weight(wk, 1, 0, "table1")
+        both = kept([P, 2 * PASS * PACK], BF16, "table1")
         for a in range(2):
-            w1_q[a, 1] = quantize_weight(round_weight(w1_raw[a, 1], 0), "w1_%d1" % a)
-        lead = kept([P, PACK, PAIRS], F32, "staging0")
+            grouped = round_weight(w1_raw[a, 1], 0, both[:, a * PASS * PACK : (a + 1) * PASS * PACK])
+            w1_q[a, 1] = quantize_weight(grouped, "w1_%d1" % a)
+        wk_raw[1] = load_weight(wk, 1, 0, "staging0")
+        lead = kept([P, PACK, PAIRS], F32, "staging1")
         nc.sync.dma_start(out=lead[:], in_=leadm.rearrange("(p t) m -> p t m", t=PACK))
         pending = []
         for c in range(CHUNKS):
             q_pass(q_acc[c], 1, 0, c)
             if c % 2 == 0:
-                logs = ring.tile([P, 2 * CHUNK, PACK], F32, name="logs", bufs=4)
+                logs = ring.tile([P, 2 * CHUNK, PACK], F32, name="logs", bufs=5, align_bytes=64)
             log_energy(q_acc[c], logs[:, c % 2 * CHUNK : (c % 2 + 1) * CHUNK, :])
             if c % 2 == 1:
                 h_bf = apply_gain(logs[:], 0)
@@ -232,7 +236,7 @@ def tile_list_spindle_lead_scores_kernel(
             for a in range(2):
                 q_pass(acc, a, 1, c)
             if c % 2 == 0:
-                logs = ring.tile([P, 2 * CHUNK, PACK], F32, name="logs", bufs=4)
+                logs = ring.tile([P, 2 * CHUNK, PACK], F32, name="logs", bufs=5, align_bytes=64)
             part = logs[:, c % 2 * CHUNK : (c % 2 + 1) * CHUNK, :]
             log_energy(acc, part)
             if c >= CHUNKS - 2:
@@ -244,7 +248,8 @@ def tile_list_spindle_lead_scores_kernel(
                 quantize_features(*pending.pop())
                 pending.append((h_bf, 1, (c - 1) * CHUNK))
             if c < 2:
-                grouped = round_weight(wk_raw[c], 0)
+                slot = ring.tile([P, PASS * PACK], BF16, name="logs", bufs=5, align_bytes=64)
+                grouped = round_weight(wk_raw[c], 0, slot[:])
                 wk_q[c] = quantize_weight(grouped, "wk_%d" % c)
             if c in (1, 2):
                 for t in range(PACK - 1):

@@ -58,21 +58,21 @@ def tile_list_spindle_lead_scores_kernel(
             nc.sync.dma_start(out=raw[:], in_=rows.rearrange("(p j) c -> p j c", j=PACK))
             return raw[:]
 
-        w1_raw = {}
-        w1_raw[0, 0] = load_weight(w1, 0, 0, "staging0")
         nc.sync.dma_start(offs_sb[:], offs)
-        w1_raw[1, 0] = load_weight(w1, 1, 0, "staging1")
-        w4_raw = kept([P, 2, N // 2], I32, "w4_raw")
-        nc.sync.dma_start(out=w4_raw[:], in_=w4_words.rearrange("a p c -> p a c").bitcast(I32))
         nc.sync.dma_start(pos1_sb[:], pos1)
         nc.sync.dma_start(pos2_sb[:], pos2)
+        w1_raw = {}
+        w1_raw[0, 0] = load_weight(w1, 0, 0, "staging0")
+        w4_raw = kept([P, 2, N // 2], I32, "w4_raw")
+        nc.sync.dma_start(out=w4_raw[:], in_=w4_words.rearrange("a p c -> p a c").bitcast(I32))
+        w1_raw[1, 0] = load_weight(w1, 1, 0, "staging1")
         table = {}
         for a in range(2):
             table[a] = kept([P, T], I32, "table%d" % a)
             nc.sync.dma_start(out=table[a][:], in_=tab_words[a].rearrange("p t i -> p (t i)").bitcast(I32))
         for q in range(4):
             for a in range(2):
-                queue = nc.gpsimd if q == 3 else nc.scalar
+                queue = nc.scalar if 2 * q + a < 5 else nc.gpsimd
                 queue.dma_start(
                     out=table_planes[32 * q + 4 * a : 32 * q + 4 * a + 4, :],
                     in_=tab_scales[a, 4 * q : 4 * q + 4, :].bitcast(I32),
@@ -85,10 +85,7 @@ def tile_list_spindle_lead_scores_kernel(
         gain_sb = kept([P, 2, PACK], F32, "gain_sb")
         nc.gpsimd.dma_start(out=gain_sb[:], in_=gain.rearrange("(b p t) -> p b t", b=2, t=PACK))
 
-        def round_weight(raw, scalar_share, grouped=None):
-            if grouped is None:
-                fresh = ring.tile([P, PASS * PACK], BF16, name="grouped", align_bytes=64)
-                grouped = fresh[:]
+        def round_weight(raw, scalar_share, grouped):
             dst = grouped.rearrange("p (t m j) -> p m t j", t=PACK, j=PACK)
             src = raw.rearrange("p j (m t) -> p m t j", t=PACK)
             if scalar_share > 0:
@@ -97,19 +94,21 @@ def tile_list_spindle_lead_scores_kernel(
                 nc.vector.tensor_copy(out=dst[:, scalar_share:, :, :], in_=src[:, scalar_share:, :, :])
             return grouped
 
-        def quantize_weight(grouped, name):
-            codes = kept([P, PASS], U32, name + "_codes")
+        def quantize_weight(grouped, name, buffer=None):
+            codes = kept([P, PASS], U32, buffer or name + "_codes")
             plane = kept([P, PASS], U8, name + "_plane")
             nc.vector.quantize_mx(out=codes[:].bitcast(FP8X4), scales=plane[:], in_=grouped)
             return codes, plane
 
         w1_q = {}
+        w1_bf = {}
         for a in range(2):
-            w1_q[a, 0] = quantize_weight(round_weight(w1_raw[a, 0], P), "w1_%d0" % a)
+            w1_bf[a] = round_weight(w1_raw[a, 0], P, kept([P, PASS * PACK], BF16, "rounded%d" % a)[:])
             w1_raw[a, 1] = load_weight(w1, a, 1, "staging%d" % a)
 
         v_planes = kept([P, S], U8, "v_planes")
         nc.vector.tensor_copy(v_planes[:], table_planes[:].bitcast(U8).indirect(offs_sb[:]))
+        w1_q[0, 0] = quantize_weight(w1_bf[0], "w1_00", "table_planes")
 
         w4_codes = kept([P, 2, 2 * N], U8, "w4_codes")
         for b in range(2):
@@ -121,7 +120,7 @@ def tile_list_spindle_lead_scores_kernel(
         def half_list(h):
             return offs_sb[:, h * HALF // 16 : (h + 1) * HALF // 16]
 
-        v_all = kept([P, 2 * S], U32, "table_planes")
+        v_all = kept([P, 2 * S], U32, "rounded0")
         v_words = {(a, h): v_all[:, a * S + h * HALF : a * S + (h + 1) * HALF] for a in range(2) for h in range(2)}
 
         def gather_words(a, h):
@@ -130,7 +129,8 @@ def tile_list_spindle_lead_scores_kernel(
         wk_raw = {}
         for h in range(2):
             gather_words(0, h)
-        w4_planes = kept([P, 2, N], U8, "table0")
+        w1_q[1, 0] = quantize_weight(w1_bf[1], "w1_10", "table0")
+        w4_planes = kept([P, 2, N], U8, "rounded1")
         nc.vector.tensor_copy(
             out=w4_planes[:].rearrange("p a (t m) -> p a t m", t=PACK),
             in_=w4_planes_raw[:].bitcast(U8).rearrange("p a (m t) -> p a t m", t=PACK),
@@ -231,14 +231,18 @@ def tile_list_spindle_lead_scores_kernel(
                 pending.append((h_bf, 0, (c - 1) * CHUNK))
 
         wk_q = {}
+        wk_bf = {}
         for c in range(CHUNKS):
-            acc = bank(c % 2)
+            acc = bank(c % 4)
             for a in range(2):
                 q_pass(acc, a, 1, c)
             if c % 2 == 0:
                 logs = ring.tile([P, 2 * CHUNK, PACK], F32, name="logs", bufs=5, align_bytes=64)
             part = logs[:, c % 2 * CHUNK : (c % 2 + 1) * CHUNK, :]
             log_energy(acc, part)
+            if c in (0, 2):
+                slot = ring.tile([P, PASS * PACK], BF16, name="logs", bufs=5, align_bytes=64)
+                wk_bf[c // 2] = round_weight(wk_raw[c // 2], 0, slot[:])
             if c >= CHUNKS - 2:
                 h_bf = apply_gain(part, 1)
                 quantize_features(*pending.pop())
@@ -247,30 +251,28 @@ def tile_list_spindle_lead_scores_kernel(
                 h_bf = apply_gain(logs[:], 1)
                 quantize_features(*pending.pop())
                 pending.append((h_bf, 1, (c - 1) * CHUNK))
-            if c < 2:
-                slot = ring.tile([P, PASS * PACK], BF16, name="logs", bufs=5, align_bytes=64)
-                grouped = round_weight(wk_raw[c], 0, slot[:])
-                wk_q[c] = quantize_weight(grouped, "wk_%d" % c)
+            if c in (1, 3):
+                wk_q[c // 2] = quantize_weight(wk_bf[c // 2], "wk_%d" % (c // 2))
             if c in (1, 2):
-                for t in range(PACK - 1):
-                    g2_acc[t, c - 1] = bank(2 + 2 * t + c - 1)
+                for t in range(2):
+                    g2_acc[t, c - 1] = bank(4 + 2 * t + c - 1)
                     g2_w4_pass(t, c - 1, 0)
             if 3 <= c < 7:
-                for t in range(PACK - 1):
+                for t in range(2):
                     g2_wk_pass(t, (c - 3) % 2, (c - 3) // 2)
             if c == CHUNKS - 1:
-                for t in range(PACK - 1):
+                for t in range(2):
                     g2_w4_pass(t, 0, 1)
         quantize_features(*pending.pop())
-        for t in range(PACK - 1):
+        for t in range(2):
             g2_w4_pass(t, 1, 1)
-        t = PACK - 1
-        for h in range(2):
-            g2_acc[t, h] = bank(h)
-            g2_w4_pass(t, h, 0)
-            for a in range(2):
-                g2_wk_pass(t, h, a)
-            g2_w4_pass(t, h, 1)
+        for t in range(2, PACK):
+            for h in range(2):
+                g2_acc[t, h] = bank(2 * (t - 2) + h)
+                g2_w4_pass(t, h, 0)
+                for a in range(2):
+                    g2_wk_pass(t, h, a)
+                g2_w4_pass(t, h, 1)
 
         g2 = [kept([P, S], F32, "g2_%d" % t) for t in range(PACK)]
         for t, h in [(0, 0), (1, 0), (0, 1), (1, 1), (2, 0), (2, 1), (3, 0), (3, 1)]:
@@ -281,15 +283,17 @@ def tile_list_spindle_lead_scores_kernel(
         y_codes = kept([P, PAIRS], I32, "y_codes")
         y_plane = kept([P, PAIRS // 4], I32, "y_plane")
 
-        def pairs(t, m0, m1):
-            left = ring.tile([P, m1 - m0], F32, name="left")
-            right = ring.tile([P, m1 - m0], F32, name="right")
-            top = ring.tile([P, m1 - m0], F32, name="top")
-            nc.vector.tensor_copy(left[:], g2[t][:].indirect(pos1_sb[:, m0 // 16 : m1 // 16]))
-            nc.vector.tensor_copy(right[:], g2[t][:].indirect(pos2_sb[:, m0 // 16 : m1 // 16]))
+        def pairs(t0, m0, m1):
+            left = ring.tile([P, 2, m1 - m0], F32, name="left", bufs=2)
+            right = ring.tile([P, 2, m1 - m0], F32, name="right", bufs=2)
+            top = ring.tile([P, 2, m1 - m0], F32, name="top", bufs=2)
+            for u in range(2):
+                nc.vector.tensor_copy(left[:, u, :], g2[t0 + u][:].indirect(pos1_sb[:, m0 // 16 : m1 // 16]))
+                nc.vector.tensor_copy(right[:, u, :], g2[t0 + u][:].indirect(pos2_sb[:, m0 // 16 : m1 // 16]))
             nc.vector.tensor_tensor(out=top[:], in0=left[:], in1=right[:], op=ALU.max)
-            nc.vector.tensor_tensor(out=y[:, t, m0:m1], in0=top[:], in1=lead[:, t, m0:m1], op=ALU.mult)
-            nc.sync.dma_start(out=y_rows[:, t, m0:m1], in_=y[:, t, m0:m1])
+            rows = slice(t0, t0 + 2)
+            nc.vector.tensor_tensor(out=y[:, rows, m0:m1], in0=top[:], in1=lead[:, rows, m0:m1], op=ALU.mult)
+            nc.sync.dma_start(out=y_rows[:, rows, m0:m1], in_=y[:, rows, m0:m1])
 
         def planes(m0, m1, on_scalar):
             y_bf = kept([P, m1 - m0, PACK], BF16, "y_bf%d" % m0)
@@ -308,10 +312,9 @@ def tile_list_spindle_lead_scores_kernel(
                 out=out_1[0, :, m0:m1, :].rearrange("p m t -> p (m t)").bitcast(I32), in_=y_codes[:, m0:m1]
             )
 
-        for t in range(PACK - 1):
-            pairs(t, 0, PAIRS)
-        pairs(PACK - 1, 0, PAIRS // 2)
-        pairs(PACK - 1, PAIRS // 2, PAIRS)
+        pairs(0, 0, PAIRS)
+        pairs(2, 0, PAIRS // 2)
+        pairs(2, PAIRS // 2, PAIRS)
         planes(0, PAIRS // 2, True)
         planes(PAIRS // 2, PAIRS, False)
         for q in range(4):

from contextlib import ExitStack

import concourse.mybir as mybir

K, H, N, T, S, PAIRS = 1024, 1024, 512, 4096, 1024, 512
FLOPS = 2 * (K * H * S + H * N * S + K * N * S)

F32 = mybir.dt.float32
BF16 = mybir.dt.bfloat16
I32 = mybir.dt.int32
U32 = mybir.dt.uint32
U16 = mybir.dt.uint16
U8 = mybir.dt.uint8
FP8X4 = mybir.dt.float8_e4m3fn_x4
FP4X4 = mybir.dt.float4_e2m1fn_x4
ACT = mybir.ActivationFunctionType
ALU = mybir.AluOpType

P = 128
PACK = 4
PASS = P * PACK
HALF = 512
CHUNK = 128
CHUNKS = S // CHUNK
BANKS = 8


def tile_list_spindle_lead_scores_kernel(
    tc, tab_words, tab_scales, offs, pos1, pos2, w1, gain, w4_words, w4_scales, wk, leadm, out_0, out_1, out_2
):
    nc = tc.nc
    with ExitStack() as ctx:
        keep = ctx.enter_context(tc.tile_pool(name="keep", bufs=1))
        ring = ctx.enter_context(tc.tile_pool(name="ring", bufs=3))
        psum = ctx.enter_context(tc.psum_pool(name="psum", bufs=1))

        def kept(shape, dtype, name):
            return keep.tile(shape, dtype, name=name, tag=name, align_bytes=64)

        def bank(i):
            return psum.tile([P, PACK, CHUNK], F32, name="bank%d" % i)

        offs_sb = keep.tile([P, S // 16], U16, name="offs_sb")
        pos1_sb = keep.tile([P, PAIRS // 16], U16, name="pos1_sb")
        pos2_sb = keep.tile([P, PAIRS // 16], U16, name="pos2_sb")
        table_planes = kept([P, T // 4], I32, "table_planes")
        w4_planes_raw = kept([P, 2, N // 4], I32, "w4_planes_raw")
        one = kept([P, 1], F32, "one")
        warm = kept([P, 1], F32, "warm")
        nc.vector.memset(one[:], 1.0)
        nc.vector.memset(table_planes[:], 0)
        nc.vector.memset(w4_planes_raw[:], 0)
        nc.scalar.activation(out=warm[:], in_=one[:], func=ACT.Ln)

        def load_weight(w, a, b, buffer):
            raw = kept([P, PACK, PASS], F32, buffer)
            rows = w[a * PASS : (a + 1) * PASS, b * PASS : (b + 1) * PASS]
            nc.sync.dma_start(out=raw[:], in_=rows.rearrange("(p j) c -> p j c", j=PACK))
            return raw[:]

        nc.sync.dma_start(offs_sb[:], offs)
        nc.sync.dma_start(pos1_sb[:], pos1)
        nc.sync.dma_start(pos2_sb[:], pos2)
        w1_raw = {}
        w1_raw[0, 0] = load_weight(w1, 0, 0, "staging0")
        w4_raw = kept([P, 2, N // 2], I32, "w4_raw")
        nc.sync.dma_start(out=w4_raw[:], in_=w4_words.rearrange("a p c -> p a c").bitcast(I32))
        w1_raw[1, 0] = load_weight(w1, 1, 0, "staging1")
        table = {}
        for a in range(2):
            table[a] = kept([P, T], I32, "table%d" % a)
            nc.sync.dma_start(out=table[a][:], in_=tab_words[a].rearrange("p t i -> p (t i)").bitcast(I32))
        for q in range(4):
            for a in range(2):
                queue = nc.scalar if 2 * q + a < 5 else nc.gpsimd
                queue.dma_start(
                    out=table_planes[32 * q + 4 * a : 32 * q + 4 * a + 4, :],
                    in_=tab_scales[a, 4 * q : 4 * q + 4, :].bitcast(I32),
                )
        for q in range(4):
            nc.gpsimd.dma_start(
                out=w4_planes_raw[32 * q : 32 * q + 4, :, :],
                in_=w4_scales[:, 4 * q : 4 * q + 4, :].rearrange("a r n -> r a n").bitcast(I32),
            )
        gain_sb = kept([P, 2, PACK], F32, "gain_sb")
        nc.gpsimd.dma_start(out=gain_sb[:], in_=gain.rearrange("(b p t) -> p b t", b=2, t=PACK))

        def round_weight(raw, scalar_share, grouped):
            dst = grouped.rearrange("p (t m j) -> p m t j", t=PACK, j=PACK)
            src = raw.rearrange("p j (m t) -> p m t j", t=PACK)
            if scalar_share > 0:
                nc.scalar.copy(out=dst[:, :scalar_share, :, :], in_=src[:, :scalar_share, :, :])
            if scalar_share < P:
                nc.vector.tensor_copy(out=dst[:, scalar_share:, :, :], in_=src[:, scalar_share:, :, :])
            return grouped

        def quantize_weight(grouped, name, buffer=None):
            codes = kept([P, PASS], U32, buffer or name + "_codes")
            plane = kept([P, PASS], U8, name + "_plane")
            nc.vector.quantize_mx(out=codes[:].bitcast(FP8X4), scales=plane[:], in_=grouped)
            return codes, plane

        w1_q = {}
        w1_bf = {}
        for a in range(2):
            w1_bf[a] = round_weight(w1_raw[a, 0], P, kept([P, PASS * PACK], BF16, "rounded%d" % a)[:])
            w1_raw[a, 1] = load_weight(w1, a, 1, "staging%d" % a)

        v_planes = kept([P, S], U8, "v_planes")
        nc.vector.tensor_copy(v_planes[:], table_planes[:].bitcast(U8).indirect(offs_sb[:]))
        w1_q[0, 0] = quantize_weight(w1_bf[0], "w1_00", "table_planes")

        w4_codes = kept([P, 2, 2 * N], U8, "w4_codes")
        for b in range(2):
            nc.vector.tensor_copy(
                out=w4_codes[:, b, :].rearrange("p (t m e) -> p t m e", t=PACK, e=2),
                in_=w4_raw[:, b, :].bitcast(U8).rearrange("p (m t e) -> p t m e", t=PACK, e=2),
            )

        def half_list(h):
            return offs_sb[:, h * HALF // 16 : (h + 1) * HALF // 16]

        v_all = kept([P, 2 * S], U32, "rounded0")
        v_words = {(a, h): v_all[:, a * S + h * HALF : a * S + (h + 1) * HALF] for a in range(2) for h in range(2)}

        def gather_words(a, h):
            nc.vector.tensor_copy(v_words[a, h], table[a][:].bitcast(U32).indirect(half_list(h)))

        wk_raw = {}
        for h in range(2):
            gather_words(0, h)
        w1_q[1, 0] = quantize_weight(w1_bf[1], "w1_10", "table0")
        w4_planes = kept([P, 2, N], U8, "rounded1")
        nc.vector.tensor_copy(
            out=w4_planes[:].rearrange("p a (t m) -> p a t m", t=PACK),
            in_=w4_planes_raw[:].bitcast(U8).rearrange("p a (m t) -> p a t m", t=PACK),
        )
        wk_raw[0] = load_weight(wk, 0, 0, "w4_planes_raw")

        def v_operand(a, h, cols):
            at = slice(h * HALF + cols.start, h * HALF + cols.stop)
            return v_words[a, h][:, cols].bitcast(FP8X4), v_planes[4 * a :, at]

        def q_pass(acc, a, b, c):
            h, cols = c // PACK, slice(c % PACK * CHUNK, (c % PACK + 1) * CHUNK)
            codes, plane = w1_q[a, b]
            rhs, rhs_scale = v_operand(a, h, cols)
            for t in range(PACK):
                nc.tensor.matmul_mx(
                    out=acc[:, t, :],
                    lhsT=codes[:, t * P : (t + 1) * P].bitcast(FP8X4),
                    lhsT_scale=plane[:, t * P : (t + 1) * P],
                    rhs=rhs,
                    rhs_scale=rhs_scale,
                    start=(a == 0 and t == 0),
                    stop=(a == 1 and t == PACK - 1),
                )

        h_codes = {(b, h): kept([P, HALF], U32, "h_codes%d%d" % (b, h)) for b in range(2) for h in range(2)}
        h_plane = {(b, h): kept([P, HALF], U8, "h_plane%d%d" % (b, h)) for b in range(2) for h in range(2)}

        def log_energy(acc, logs):
            squares = ring.tile([P, CHUNK, PACK], F32, name="squares")
            nc.scalar.activation(out=squares[:], in_=acc[:].rearrange("p t j -> p j t"), func=ACT.Square)
            nc.scalar.activation(out=logs, in_=squares[:], func=ACT.Ln, bias=1.0)

        def apply_gain(logs, b):
            width = logs.shape[1]
            h_bf = ring.tile([P, width, PACK], BF16, name="h_bf", align_bytes=64)
            nc.vector.tensor_tensor(
                out=h_bf[:], in0=logs, in1=gain_sb[:, b : b + 1, :].to_broadcast([P, width, PACK]), op=ALU.mult
            )
            return h_bf

        def quantize_features(h_bf, b, j0):
            h, cols = j0 // HALF, slice(j0 % HALF, j0 % HALF + h_bf.shape[1])
            nc.vector.quantize_mx(
                out=h_codes[b, h][:, cols].bitcast(FP8X4),
                scales=h_plane[b, h][:, cols],
                in_=h_bf[:].rearrange("p j t -> p (j t)"),
            )

        g2_acc = {}

        def g2_w4_pass(t, h, b):
            nc.tensor.matmul_mx(
                out=g2_acc[t, h][:].rearrange("p t j -> p (t j)"),
                lhsT=w4_codes[:, b, 2 * t * P : 2 * (t + 1) * P].bitcast(FP4X4),
                lhsT_scale=w4_planes[:, b, t * P : (t + 1) * P],
                rhs=h_codes[b, h][:].bitcast(FP8X4),
                rhs_scale=h_plane[b, h][:],
                start=(b == 0),
                stop=(b == 1),
            )

        def g2_wk_pass(t, h, a):
            codes, plane = wk_q[a]
            rhs, rhs_scale = v_operand(a, h, slice(0, HALF))
            nc.tensor.matmul_mx(
                out=g2_acc[t, h][:].rearrange("p t j -> p (t j)"),
                lhsT=codes[:, t * P : (t + 1) * P].bitcast(FP8X4),
                lhsT_scale=plane[:, t * P : (t + 1) * P],
                rhs=rhs,
                rhs_scale=rhs_scale,
                start=False,
                stop=False,
            )

        q_acc = [bank(c) for c in range(CHUNKS)]
        for c in range(CHUNKS):
            q_pass(q_acc[c], 0, 0, c)
        for h in range(2):
            gather_words(1, h)
        both = kept([P, 2 * PASS * PACK], BF16, "table1")
        for a in range(2):
            grouped = round_weight(w1_raw[a, 1], 0, both[:, a * PASS * PACK : (a + 1) * PASS * PACK])
            w1_q[a, 1] = quantize_weight(grouped, "w1_%d1" % a)
        wk_raw[1] = load_weight(wk, 1, 0, "staging0")
        lead = kept([P, PACK, PAIRS], F32, "staging1")
        nc.sync.dma_start(out=lead[:], in_=leadm.rearrange("(p t) m -> p t m", t=PACK))
        pending = []
        for c in range(CHUNKS):
            q_pass(q_acc[c], 1, 0, c)
            if c % 2 == 0:
                logs = ring.tile([P, 2 * CHUNK, PACK], F32, name="logs", bufs=5, align_bytes=64)
            log_energy(q_acc[c], logs[:, c % 2 * CHUNK : (c % 2 + 1) * CHUNK, :])
            if c % 2 == 1:
                h_bf = apply_gain(logs[:], 0)
                if pending:
                    quantize_features(*pending.pop())
                pending.append((h_bf, 0, (c - 1) * CHUNK))

        wk_q = {}
        wk_bf = {}
        for c in range(CHUNKS):
            acc = bank(c % 4)
            for a in range(2):
                q_pass(acc, a, 1, c)
            if c % 2 == 0:
                logs = ring.tile([P, 2 * CHUNK, PACK], F32, name="logs", bufs=5, align_bytes=64)
            part = logs[:, c % 2 * CHUNK : (c % 2 + 1) * CHUNK, :]
            log_energy(acc, part)
            if c in (0, 2):
                slot = ring.tile([P, PASS * PACK], BF16, name="logs", bufs=5, align_bytes=64)
                wk_bf[c // 2] = round_weight(wk_raw[c // 2], 0, slot[:])
            if c >= CHUNKS - 2:
                h_bf = apply_gain(part, 1)
                quantize_features(*pending.pop())
                pending.append((h_bf, 1, c * CHUNK))
            elif c % 2 == 1:
                h_bf = apply_gain(logs[:], 1)
                quantize_features(*pending.pop())
                pending.append((h_bf, 1, (c - 1) * CHUNK))
            if c in (1, 3):
                wk_q[c // 2] = quantize_weight(wk_bf[c // 2], "wk_%d" % (c // 2))
            if c in (1, 2):
                for t in range(2):
                    g2_acc[t, c - 1] = bank(4 + 2 * t + c - 1)
                    g2_w4_pass(t, c - 1, 0)
            if 3 <= c < 7:
                for t in range(2):
                    g2_wk_pass(t, (c - 3) % 2, (c - 3) // 2)
            if c == CHUNKS - 1:
                for t in range(2):
                    g2_w4_pass(t, 0, 1)
        quantize_features(*pending.pop())
        for t in range(2):
            g2_w4_pass(t, 1, 1)
        for t in range(2, PACK):
            for h in range(2):
                g2_acc[t, h] = bank(2 * (t - 2) + h)
                g2_w4_pass(t, h, 0)
                for a in range(2):
                    g2_wk_pass(t, h, a)
                g2_w4_pass(t, h, 1)

        g2 = [kept([P, S], F32, "g2_%d" % t) for t in range(PACK)]
        for t, h in [(0, 0), (1, 0), (0, 1), (1, 1), (2, 0), (2, 1), (3, 0), (3, 1)]:
            nc.scalar.copy(out=g2[t][:, h * HALF : (h + 1) * HALF], in_=g2_acc[t, h][:].rearrange("p t j -> p (t j)"))

        y = kept([P, PACK, PAIRS], F32, "y")
        y_rows = out_0.rearrange("(p t) m -> p t m", t=PACK)
        y_codes = kept([P, PAIRS], I32, "y_codes")
        y_plane = kept([P, PAIRS // 4], I32, "y_plane")

        def pairs(t0, m0, m1):
            left = ring.tile([P, 2, m1 - m0], F32, name="left", bufs=2)
            right = ring.tile([P, 2, m1 - m0], F32, name="right", bufs=2)
            top = ring.tile([P, 2, m1 - m0], F32, name="top", bufs=2)
            for u in range(2):
                nc.vector.tensor_copy(left[:, u, :], g2[t0 + u][:].indirect(pos1_sb[:, m0 // 16 : m1 // 16]))
                nc.vector.tensor_copy(right[:, u, :], g2[t0 + u][:].indirect(pos2_sb[:, m0 // 16 : m1 // 16]))
            nc.vector.tensor_tensor(out=top[:], in0=left[:], in1=right[:], op=ALU.max)
            rows = slice(t0, t0 + 2)
            nc.vector.tensor_tensor(out=y[:, rows, m0:m1], in0=top[:], in1=lead[:, rows, m0:m1], op=ALU.mult)
            nc.sync.dma_start(out=y_rows[:, rows, m0:m1], in_=y[:, rows, m0:m1])

        def planes(m0, m1, on_scalar):
            y_bf = kept([P, m1 - m0, PACK], BF16, "y_bf%d" % m0)
            dst = y_bf[:]
            src = y[:, :, m0:m1].rearrange("p t m -> p m t")
            if on_scalar:
                nc.scalar.copy(out=dst, in_=src)
            else:
                nc.vector.tensor_copy(out=dst, in_=src)
            nc.vector.quantize_mx(
                out=y_codes[:, m0:m1].bitcast(FP8X4),
                scales=y_plane[:].bitcast(U8)[:, m0:m1],
                in_=y_bf[:].rearrange("p m t -> p (m t)"),
            )
            nc.sync.dma_start(
                out=out_1[0, :, m0:m1, :].rearrange("p m t -> p (m t)").bitcast(I32), in_=y_codes[:, m0:m1]
            )

        pairs(0, 0, PAIRS)
        pairs(2, 0, PAIRS // 2)
        pairs(2, PAIRS // 2, PAIRS)
        planes(0, PAIRS // 2, True)
        planes(PAIRS // 2, PAIRS, False)
        for q in range(4):
            nc.scalar.dma_start(
                out=out_2[0, 4 * q : 4 * q + 4, :].bitcast(I32), in_=y_plane[32 * q : 32 * q + 4, :]
            )
